import numpy as np, ml_dtypes
CORES = [61,69,101,62,70,102]
N = 6
DEG, TK = 2, 256
MASK = [[4,0],[4,1],[4,2],[4,3],[4,0],[4,5]]
def setup_inputs(rng):
    return {"x": rng.standard_normal((N, 128, TK), dtype=np.float32).astype(ml_dtypes.bfloat16), "w": rng.standard_normal((N, 128, DEG * 128), dtype=np.float32).astype(ml_dtypes.bfloat16)}
def setup_inputs_big(rng):
    d = setup_inputs(rng)
    for k in ("x", "w"): d[k] = (d[k].astype(np.float32) * 1024.0).astype(d[k].dtype)
    return d
def setup_inputs_small(rng):
    d = setup_inputs(rng)
    for k in ("x", "w"): d[k] = (d[k].astype(np.float32) * (1 / 1024.0)).astype(d[k].dtype)
    return d
def setup_inputs_apart(rng):
    d = setup_inputs(rng)
    f = (10.0 ** rng.permutation(np.linspace(-1.5, 1.5, N))).astype(np.float32).reshape(N, 1, 1)
    for k in ("x", "w"): d[k] = (d[k].astype(np.float32) * f).astype(d[k].dtype)
    return d
def reference(x, w):
    X, W = x.astype(np.float64), w.astype(np.float64)
    y = np.zeros((N, 128, TK))
    for r in range(N):
        for i, j in enumerate(MASK[r]):
            y[r] += W[r][:, 128 * i:128 * i + 128].T @ X[j]
    return {"y": y.astype(ml_dtypes.bfloat16 if x.dtype != np.float64 else np.float64)}

from concourse.bass import DstId, RemoteDMATransfer

SCRATCH = {
    "xs": ("sbuf", [128, 256], "bfloat16"),
    "ws": ("sbuf", [128, 256], "bfloat16"),
    "xr0": ("sbuf", [128, 256], "bfloat16"),
    "xr1": ("sbuf", [128, 256], "bfloat16"),
    "ys": ("sbuf", [128, 256], "bfloat16"),
    "xd": ("dram", [128, 256], "bfloat16"),
    "acc": ("psum", [128, 256], "float32"),
}
SEMAPHORES = ["sx", "sw", "sd", "rel", "arr", "snt", "mm", "cp", "st"]


def _bits(mask):
    return [1 << b for b in range(mask.bit_length()) if (mask >> b) & 1]


def _join(bits):
    m = 0
    for b in bits:
        m |= b
    return m


def _pow2(n):
    p = 1
    while p * 2 <= n:
        p *= 2
    return p


def _plan(T, topo):
    cores = list(T.cores)
    table = T.tables["MASK"]
    wants = {}
    for r, row in enumerate(table):
        for i, j in enumerate(row):
            if j != r:
                wants.setdefault(cores[j], []).append((cores[r], i))
    taken = set(cores)
    calls = {}
    hand = {}
    relay = {}
    expect = {}
    for s, lst in wants.items():
        far, near = {}, []
        for d, i in lst:
            if not topo.may_write(s, d):
                cand = [c for c in range(topo.CHIPS * topo.CORES_PER_CHIP)
                        if topo.chip(c) == topo.chip(s) and c not in taken and topo.may_write(c, d)]
                cand.sort(key=lambda c: (topo.die(c) != topo.die(s), c))
                v = cand[0]
                taken.add(v)
                m_in = _join(_bits(topo.mask(s, v))[:8])
                m_out = topo.mask(v, d)
                hand.setdefault(s, []).append((v, m_in))
                relay[v] = (len(_bits(m_in)), d, i, m_out)
                expect[d] = expect.get(d, 0) + len(_bits(m_out))
            elif topo.chip(d) != topo.chip(s):
                far.setdefault(topo.chip(d), []).append((d, i))
            else:
                near.append((d, i))
        out = []
        busy = 0
        if far:
            ok = ~0
            for grp in far.values():
                for d, _ in grp:
                    ok &= topo.mask(s, d)
            eng = _bits(ok)
            per = _pow2(len(eng) // len(far))
            order = sorted(far, key=lambda ch: (topo.same_plane(topo.chip(s), ch) or topo.mates(topo.chip(s), ch), ch))
            call = []
            for k, ch in enumerate(order):
                m = _join(eng[k * per:(k + 1) * per])
                busy |= m
                call.append((m, far[ch]))
            out.append(call)
        if near:
            ok = ~0
            for d, _ in near:
                ok &= topo.mask(s, d)
            eng = _bits(ok & ~busy) or _bits(ok)
            out.append([(_join(eng[:_pow2(min(8, len(eng)))]), near)])
        for call in out:
            for m, grp in call:
                for d, _ in grp:
                    expect[d] = expect.get(d, 0) + len(_bits(m))
        if out:
            calls[s] = out
    return calls, hand, relay, expect


def rank_program(g, core, T, topo):
    calls, hand, relay, expect = _plan(T, topo)
    S = T.sem

    if core in relay:
        n_in, d, i, m = relay[core]
        rid, pid, _ = topo.addr(d)
        g.wait_ge(S.rel, n_in)
        g.remote_dma(out_ap=T["xr%d" % i][:], in_ap=T.xd[:], remote_sem=S.arr, local_sem=S.snt,
                     pid=pid, routing_id=rid, dma_engine_mask=m)
        g.wait_ge(S.snt, len(_bits(m)))
        return

    rank = T.rank_of(core)
    if rank is None:
        return
    row = T.tables["MASK"][rank]

    left = 0
    if core in hand:
        g.sync.dma_start(T.xd[:], T.x[:]).then_inc(S.sd, 16)
        g.wait_ge(S.sd, 16)
        for v, m in hand[core]:
            rid, pid, _ = topo.addr(v)
            g.remote_dma(out_ap=T.xd[:], in_ap=T.xd[:], remote_sem=S.rel, local_sem=S.snt,
                         pid=pid, routing_id=rid, dma_engine_mask=m)
            left += len(_bits(m))
        g.sync.wait_ge(S.snt, left)
        g.scalar.wait_ge(S.snt, left)
    g.sync.dma_start(T.xs[:], T.x[:]).then_inc(S.sx, 16)
    if core in calls:
        g.scalar.wait_ge(S.sx, 16)
    g.scalar.dma_start(T.ws[:], T.w[:]).then_inc(S.sw, 16)
    if core in calls:
        g.wait_ge(S.sx, 16)
        for call in calls[core]:
            trs = []
            for m, grp in call:
                ids = []
                for d, _ in grp:
                    rid, pid, _se = topo.addr(d)
                    ids.append(DstId(rid=rid, pnc=pid))
                trs.append(RemoteDMATransfer(dst_ids=ids, dma_engine_mask=m, remote_sem=S.arr,
                                             srcs=[T.xs[:]], dsts=[T["xr%d" % i][:] for _, i in grp]))
                left += len(_bits(m))
            g.remote_dma_fused(trs, local_sem=S.snt)
        g.wait_ge(S.snt, left)

    own = [i for i, j in enumerate(row) if j == rank]
    got = [i for i, j in enumerate(row) if j != rank]
    todo = [(i, T.xs) for i in own] + [(i, T["xr%d" % i]) for i in got]
    g.tensor.wait_ge(S.sw, 16)
    if own:
        g.tensor.wait_ge(S.sx, 16)
    for k, (i, xb) in enumerate(todo):
        if got and k == len(own):
            g.tensor.wait_ge(S.arr, expect[core])
        mmi = g.tensor.matmul(T.acc[:], T.ws[:, 128 * i:128 * i + 128], xb[:], k == 0, k == len(todo) - 1)
    mmi.then_inc(S.mm, 1)
    if not own:
        g.tensor.wait_ge(S.sx, 16)

    g.vector.wait_ge(S.mm, 1)
    g.vector.tensor_copy(T.ys[:], T.acc[:]).then_inc(S.cp, 1)
    g.sync.wait_ge(S.cp, 1)
    g.sync.dma_start(T.y[:], T.ys[:]).then_inc(S.st, 16)
    g.sync.wait_ge(S.st, 16)
